import numpy as np
import ml_dtypes


def mxq(x, axis, fmt="e4m3"):
    dtype, down = {"e4m3": (ml_dtypes.float8_e4m3fn, 7), "e5m2": (ml_dtypes.float8_e5m2, 14)}[fmt]
    v = np.moveaxis(np.asarray(x, np.float32).astype(ml_dtypes.bfloat16).astype(np.float64), axis, -1)
    blocks = v.reshape(v.shape[:-1] + (-1, 32))
    amax = np.abs(blocks).max(-1, keepdims=True)
    byte = np.maximum(np.where(amax > 0, np.frexp(amax)[1] - 1 + 127, 0) - down, 1)
    scale = np.exp2(byte - 127.0)
    codes = (blocks / scale).astype(np.float32).astype(dtype).astype(np.float64)
    return np.moveaxis((codes * scale).reshape(v.shape), -1, axis)


WIDE = False


def mx_kscale(k):
    if not WIDE:
        return np.ones(k)
    levels = np.array([10, -10, 5, -5, 0])
    if k % 512:
        return np.exp2(np.random.permutation(np.resize(levels, k // 32))).repeat(32)
    a = np.empty((k // 512, 16))
    for p in range(k // 512):
        a[p, :8] = np.random.permutation(np.resize(levels, 8))
        for g in range(8):
            far = levels[np.abs(levels - a[p, g]) >= 10]
            a[p, g + 8] = far[np.random.randint(len(far))]
    return np.exp2(a.ravel()).repeat(32)


def f64(x):
    return np.asarray(x).astype(np.float64)


def striped(idx):
    return np.tile(idx.reshape(-1, 16).T, (8, 1)).astype(np.uint16)


def unstriped(offs):
    return offs[:16].T.reshape(-1).astype(np.int64)


def striped8(idx):
    return np.concatenate([x.reshape(-1, 16).T for x in idx]).astype(np.uint16)


def runs(offs, k):
    lists = np.stack([offs[16 * r : 16 * r + 16].T.reshape(-1) for r in range(8)]).astype(np.int64)
    return lists[np.arange(k) % 512 // 64]


def pack_weight(w):
    k, n = w.shape
    w = f64(np.asarray(w, np.float32).astype(ml_dtypes.bfloat16)).reshape(k // 32, 32, n)
    amax = np.abs(w).max(1)
    byte = np.clip(np.where(amax > 0, np.frexp(amax)[1] - 1 + 127 - 7, 1), 1, 254)
    scaled = (w * np.exp2(127.0 - byte)[:, None, :]).reshape(k, n).astype(np.float32)
    words = np.ascontiguousarray(scaled.reshape(k // 512, 128, 4, n).transpose(0, 1, 3, 2)).astype(ml_dtypes.float8_e4m3fn).view(np.uint8)
    return words, np.ascontiguousarray(byte.astype(np.uint8).reshape(k // 512, 16, n))


def unpack_weight(words, scales):
    g, p, n, _ = words.shape
    vals = np.ascontiguousarray(words).view(ml_dtypes.float8_e4m3fn).astype(np.float64) * np.repeat(np.exp2(scales.astype(np.float64) - 127.0), 8, axis=1)[..., None]
    return vals.transpose(0, 1, 3, 2).reshape(g * 512, n)


E2M1 = np.array([0.0, 0.5, 1.0, 1.5, 2.0, 3.0, 4.0, 6.0, -0.0, -0.5, -1.0, -1.5, -2.0, -3.0, -4.0, -6.0])


def pack_fp4(w):
    k, n = w.shape
    w = f64(np.asarray(w, np.float32).astype(ml_dtypes.bfloat16)).reshape(k // 32, 32, n)
    amax = np.abs(w).max(1)
    mant, ex = np.frexp(amax / 6.0)
    byte = np.clip(np.where(amax > 0, np.where(mant > 0.5, ex, ex - 1) + 127, 1), 1, 254)
    scaled = (w * np.exp2(127.0 - byte)[:, None, :]).reshape(k, n).astype(np.float32)
    c = np.ascontiguousarray(scaled.reshape(k // 512, 128, 4, n).transpose(0, 1, 3, 2)).astype(ml_dtypes.float4_e2m1fn).view(np.uint8) & 0xF
    words = (c[..., 0::2] | (c[..., 1::2] << 4)).reshape(k // 512, 128, 2 * n)
    return np.ascontiguousarray(words), np.ascontiguousarray(byte.astype(np.uint8).reshape(k // 512, 16, n))


def unpack_fp4(words, scales):
    g, _, n = scales.shape
    words = np.ascontiguousarray(words).reshape(g, 128, n, 2)
    nib = np.empty((g, 128, n, 4), np.uint8)
    nib[..., 0::2] = words & 0xF
    nib[..., 1::2] = words >> 4
    vals = E2M1[nib] * np.repeat(np.exp2(scales.astype(np.float64) - 127.0), 8, axis=1)[..., None]
    return vals.transpose(0, 1, 3, 2).reshape(g * 512, n)


def planes(y):
    n, m = y.shape
    v = y.astype(np.float32).astype(ml_dtypes.bfloat16).astype(np.float64).reshape(n // 32, 32, m)
    top = np.abs(v).max(1)
    byte = np.clip(np.where(top > 0, np.frexp(top)[1] - 1 + 127 - 7, 1), 1, 254)
    codes = (v * np.exp2(127.0 - byte)[:, None, :]).reshape(n, m).astype(np.float32).astype(ml_dtypes.float8_e4m3fn).view(np.uint8)
    words = codes.reshape(n // 512, 128, 4, m).transpose(0, 1, 3, 2)
    return np.ascontiguousarray(words), np.ascontiguousarray(byte.astype(np.uint8).reshape(n // 512, 16, m))


K, T, S, V, H = 512, 2048, 512, 512, 512


def setup_inputs():
    n = np.random.standard_normal
    s = mx_kscale(K)[:, None]
    u = mx_kscale(S)
    packed_xT = pack_weight(n((K, T)) * s)
    packed_w1 = pack_fp4(n((K, H)) / np.sqrt(K) / s)
    packed_w2 = pack_fp4(n((K, H)) / np.sqrt(K) / s)
    packed_w3 = pack_fp4(n((K, H)) / np.sqrt(K) / s)
    return {
        "x_words": packed_xT[0],
        "x_scales": packed_xT[1],
        "w1_words": packed_w1[0],
        "w1_scales": packed_w1[1],
        "w2_words": packed_w2[0],
        "w2_scales": packed_w2[1],
        "w3_words": packed_w3[0],
        "w3_scales": packed_w3[1],
        "ga": (np.random.uniform(0.5, 1.5, (H, 1)) * u[:, None]).astype(np.float32),
        "gb": (np.random.uniform(0.5, 1.5, (H, 1)) / u[:, None]).astype(np.float32),
        "offs": striped(np.random.permutation(T)[:S]),
        "two": striped(np.random.permutation(T)[:S]),
        "n1": striped8(np.stack([np.random.permutation(S) for _ in range(8)])),
        "n2": striped8(np.stack([np.random.permutation(S) for _ in range(8)])),
        "three": striped(np.random.permutation(T)[:V]),
        "n3": striped8(np.stack([np.random.permutation(V) for _ in range(8)])),
        "n4": striped8(np.stack([np.random.permutation(V) for _ in range(8)])),
        "n5": striped8(np.stack([np.random.permutation(V) for _ in range(8)])),
        "n6": striped8(np.stack([np.random.permutation(V) for _ in range(8)])),
    }


def reference(x_words, x_scales, w1_words, w1_scales, w2_words, w2_scales, w3_words, w3_scales, ga, gb, offs, two, n1, n2, three, n3, n4, n5, n6):
    xq = unpack_weight(x_words, x_scales)[:, unstriped(offs)]
    y = unpack_fp4(w1_words, w1_scales).T @ xq
    x_two = unpack_weight(x_words, x_scales)[:, unstriped(two)]
    d = unpack_fp4(w2_words, w2_scales).T @ x_two
    z = f64(ga) * ((y - (y[np.arange(H)[:, None], runs(n1, H)])) / (np.abs(d) + np.abs(d[np.arange(H)[:, None], runs(n2, H)]) + 0.5))
    x_three = unpack_weight(x_words, x_scales)[:, unstriped(three)]
    b = unpack_fp4(w3_words, w3_scales).T @ x_three
    pa = b[np.arange(H)[:, None], runs(n3, H)]
    kr = np.exp(-0.5 * ((b - pa) ** 2))
    pb = b[np.arange(H)[:, None], runs(n4, H)]
    kr2 = np.exp(-0.5 * ((b - pb) ** 2))
    z2 = f64(gb) * ((kr * pa + kr2 * pb) / (kr + kr2 + 0.5))
    s = 0.0625 * ((mxq(z, 0, "e4m3").T @ mxq(z2, 0, "e4m3")))
    out_0 = s[np.arange(S)[:, None], runs(n5, S)] + 0.75 * (s[np.arange(S)[:, None], runs(n6, S)])
    return (out_0,) + planes(out_0)

@@ -1,0 +1,261 @@
+from contextlib import ExitStack
+
+import concourse.mybir as mybir
+from concourse.masks import make_identity
+
+F32 = mybir.dt.float32
+BF16 = mybir.dt.bfloat16
+I32 = mybir.dt.int32
+U32 = mybir.dt.uint32
+U16 = mybir.dt.uint16
+U8 = mybir.dt.uint8
+FP8X4 = mybir.dt.float8_e4m3fn_x4
+FP4X4 = mybir.dt.float4_e2m1fn_x4
+ACT = mybir.ActivationFunctionType
+ALU = mybir.AluOpType
+
+P = 128
+N = 512
+T = 2048
+PACK = 4
+HALF = N // 2
+
+FLOPS = 4 * 2 * N * N * N
+
+
+def tile_picked_twknormbkernsum_none_po_kernel(
+    tc, x_words, x_scales, w1_words, w1_scales, w2_words, w2_scales, w3_words, w3_scales,
+    ga, gb, offs, two, n1, n2, three, n3, n4, n5, n6, out_0, out_1, out_2,
+):
+    nc = tc.nc
+    with ExitStack() as ctx:
+        keep = ctx.enter_context(tc.tile_pool(name="keep", bufs=1))
+        psum = ctx.enter_context(tc.psum_pool(name="psum", bufs=8))
+
+        def sb(name, shape, dtype):
+            return keep.tile(shape, dtype, name=name, align_bytes=64)
+
+        def bank(name):
+            return psum.tile([P, N], F32, name=name, tag="bank")
+
+        def load_list(name, ap):
+            tile = sb(name, [P, N // 16], U16)
+            nc.sync.dma_start(tile[:], ap)
+            return tile
+
+        def load_scale_rows(queue, tile, scales):
+            rows = scales[0].bitcast(I32)
+            for q in range(4):
+                queue.dma_start(tile[32 * q : 32 * q + 4, :].bitcast(I32), rows[4 * q : 4 * q + 4, :])
+
+        xs = sb("xs", [P, T], U8)
+        nc.gpsimd.memset(xs[:].bitcast(I32), 0)
+        ws_raw = [sb(f"ws_raw{i}", [P, N], U8) for i in range(3)]
+        for tile in ws_raw:
+            nc.gpsimd.memset(tile[:].bitcast(I32), 0)
+        warm = sb("warm", [P, 1], F32)
+        nc.vector.memset(warm[:], 0.0)
+        nc.scalar.activation(warm[:], warm[:], ACT.Exp)
+
+        load_scale_rows(nc.sync, xs, x_scales)
+        l_three = load_list("l_three", three)
+        l_two = load_list("l_two", two)
+        l_offs = load_list("l_offs", offs)
+        xw = sb("xw", [P, T], U32)
+        nc.sync.dma_start(xw[:].bitcast(I32), x_words[0].rearrange("p n t -> p (n t)").bitcast(I32))
+
+        ww_raw = [sb(f"ww_raw{i}", [P, 2 * N], U8) for i in range(3)]
+
+        def load_weight(i, words, scales):
+            nc.sync.dma_start(ww_raw[i][:].bitcast(I32), words[0].bitcast(I32))
+            load_scale_rows(nc.sync, ws_raw[i], scales)
+
+        load_weight(0, w3_words, w3_scales)
+        l_n3 = load_list("l_n3", n3)
+        l_n4 = load_list("l_n4", n4)
+        load_weight(1, w2_words, w2_scales)
+        gain_rows = sb("gain_rows", [P, P], F32)
+        nc.gpsimd.memset(gain_rows[:], 0.0)
+        for i, gain in enumerate((ga, gb)):
+            nc.sync.dma_start(
+                gain_rows[4 * i : 4 * i + 4, :].rearrange("t (g r) -> t g r", r=8),
+                gain.rearrange("(g t r) o -> t g (r o)", t=4, r=8),
+            )
+        load_weight(2, w1_words, w1_scales)
+        l_n2 = load_list("l_n2", n2)
+        l_n1 = load_list("l_n1", n1)
+        l_n6 = load_list("l_n6", n6)
+        l_n5 = load_list("l_n5", n5)
+
+        ident = sb("ident", [P, P], F32)
+        make_identity(nc, ident[:])
+        win_b = [sb(f"win_b{t}", [P, 2 * N], F32) for t in range(PACK)]
+        for t in range(PACK):
+            nc.gpsimd.memset(win_b[t][:, N:], 0.0)
+
+        def pick_scales(name, lst):
+            tile = sb(name, [P, N], U8)
+            nc.vector.tensor_copy(tile[:], xs[:].indirect(lst[:]))
+            return tile
+
+        def pick_words(name, lst):
+            tile = sb(name, [P, N], U32)
+            nc.vector.tensor_copy(tile[:], xw[:].indirect(lst[:]))
+            return tile
+
+        def deal(i):
+            words = sb(f"ww{i}", [P, 2 * N], U8)
+            scales = sb(f"ws{i}", [P, N], U8)
+            for dst, src in ((words, ww_raw[i]), (scales, ws_raw[i])):
+                nc.vector.tensor_copy(
+                    dst[:].bitcast(I32).rearrange("p (t g e) -> p t g e", t=4, g=16),
+                    src[:].bitcast(I32).rearrange("p (g t e) -> p t g e", t=4, g=16),
+                )
+            return words, scales
+
+        def project(name, weight, xq, xq_scales):
+            words, scales = weight
+            banks = []
+            for t in range(PACK):
+                acc = bank(f"{name}{t}")
+                nc.tensor.matmul_mx(
+                    acc[:],
+                    lhsT=words[:, 256 * t : 256 * (t + 1)].bitcast(FP4X4),
+                    lhsT_scale=scales[:, P * t : P * (t + 1)],
+                    rhs=xq[:].bitcast(FP8X4),
+                    rhs_scale=xq_scales[:],
+                    start=True,
+                    stop=True,
+                )
+                banks.append(acc)
+            return banks
+
+        s_three = pick_scales("s_three", l_three)
+        s_two = pick_scales("s_two", l_two)
+        s_offs = pick_scales("s_offs", l_offs)
+        w3q = deal(0)
+        x_three = pick_words("x_three", l_three)
+        b_ps = project("b", w3q, x_three, s_three)
+        for t in range(PACK):
+            nc.scalar.copy(win_b[t][:, :N], b_ps[t][:])
+
+        w2q = deal(1)
+        x_two = pick_words("x_two", l_two)
+        d_ps = project("d", w2q, x_two, s_two)
+        w1q = deal(2)
+        x_offs = pick_words("x_offs", l_offs)
+
+        gain_ps = bank("gain_ps")
+        nc.tensor.transpose(gain_ps[:, :P], gain_rows[:], ident[:])
+        gains = sb("gains", [P, 8], F32)
+        nc.scalar.activation(gains[:, 0:4], gain_ps[:, 0:4], ACT.Copy, scale=-1.0)
+        nc.scalar.copy(gains[:, 4:8], gain_ps[:, 4:8])
+
+        y_ps = project("y", w1q, x_offs, s_offs)
+
+        win_d = [sb(f"win_d{t}", [P, 2 * N], F32) for t in range(PACK)]
+        win_y = [sb(f"win_y{t}", [P, 2 * N], F32) for t in range(PACK)]
+
+        pa = sb("pa", [P, PACK, N], F32)
+        pb = sb("pb", [P, PACK, N], F32)
+        ka = sb("ka", [P, PACK, N], F32)
+        kb = sb("kb", [P, PACK, N], F32)
+        sq = sb("sq", [P, PACK, N], F32)
+
+        def neighbours(picked, kern, lst, t):
+            nc.vector.tensor_copy(picked[:, t, :], win_b[t][:].indirect(lst[:]))
+            nc.vector.tensor_tensor(kern[:, t, :], picked[:, t, :], win_b[t][:, :N], ALU.subtract)
+            nc.scalar.activation(sq[:, t, :], kern[:, t, :], ACT.Square)
+            nc.scalar.activation(kern[:, t, :], sq[:, t, :], ACT.Exp, scale=-0.5)
+
+        for t in range(PACK):
+            nc.scalar.activation(win_d[t][:, :N], d_ps[t][:], ACT.Abs)
+            nc.scalar.activation(win_d[t ^ 1][:, N:], d_ps[t][:], ACT.Abs)
+        for t in range(PACK):
+            neighbours(pa, ka, l_n3, t)
+        for t in range(PACK):
+            nc.scalar.activation(win_y[t][:, :N], y_ps[t][:], ACT.Copy, scale=gains[:, t : t + 1])
+            nc.scalar.activation(win_y[t ^ 1][:, N:], y_ps[t][:], ACT.Copy, scale=gains[:, t : t + 1])
+        for t in range(PACK):
+            neighbours(pb, kb, l_n4, t)
+
+        den = sb("den", [P, PACK, N], F32)
+        num = sb("num", [P, PACK, N], F32)
+        for t in range(PACK):
+            nc.vector.tensor_tensor(den[:, t, :], win_d[t][:].indirect(l_n2[:]), win_d[t ^ 1][:, N:], ALU.add)
+        for t in range(PACK):
+            nc.vector.scalar_tensor_tensor(pa[:, t, :], pa[:, t, :], gains[:, 4 + t : 5 + t], ka[:, t, :], ALU.mult, ALU.mult)
+        nc.vector.tensor_tensor(ka[:], ka[:], kb[:], ALU.add)
+        nc.scalar.activation(ka[:], ka[:], ACT.Abs_reciprocal_sqrt, bias=0.5)
+        nc.scalar.activation(ka[:], ka[:], ACT.Square)
+        nc.scalar.activation(sq[:], den[:], ACT.Abs_reciprocal_sqrt, bias=0.5)
+        nc.scalar.activation(sq[:], sq[:], ACT.Square)
+        for t in range(PACK):
+            nc.vector.scalar_tensor_tensor(pb[:, t, :], pb[:, t, :], gains[:, 4 + t : 5 + t], kb[:, t, :], ALU.mult, ALU.mult)
+        nc.vector.tensor_tensor(pa[:], pa[:], pb[:], ALU.add)
+        for t in range(PACK):
+            nc.vector.tensor_tensor(num[:, t, :], win_y[t][:].indirect(l_n1[:]), win_y[t ^ 1][:, N:], ALU.subtract)
+
+        z2_bf = sb("z2_bf", [P, PACK * N], BF16)
+        nc.vector.tensor_tensor(
+            z2_bf[:].rearrange("p (c i t) -> p c t i", i=4, t=4),
+            pa[:].rearrange("p t (c i) -> p c t i", i=4),
+            ka[:].rearrange("p t (c i) -> p c t i", i=4),
+            ALU.mult,
+        )
+        z_bf = sb("z_bf", [P, PACK * N], BF16)
+        nc.vector.tensor_tensor(
+            z_bf[:].rearrange("p (i c t) -> p c t i", i=4, t=4),
+            num[:].rearrange("p t (c i) -> p c t i", i=4),
+            sq[:].rearrange("p t (c i) -> p c t i", i=4),
+            ALU.mult,
+        )
+        z2_codes = sb("z2_codes", [P, N], U32)
+        z2_scales = sb("z2_scales", [P, N], U8)
+        nc.vector.quantize_mx(z2_codes[:].bitcast(FP8X4), z2_scales[:], z2_bf[:])
+        win_s = []
+        for i in range(PACK):
+            z_codes = sb(f"z_codes{i}", [P, P], U32)
+            z_scales = sb(f"z_scales{i}", [P, P], U8)
+            nc.vector.quantize_mx(z_codes[:].bitcast(FP8X4), z_scales[:], z_bf[:, N * i : N * (i + 1)])
+            acc = bank(f"s{i}")
+            nc.tensor.matmul_mx(
+                acc[:],
+                lhsT=z_codes[:].bitcast(FP8X4),
+                lhsT_scale=z_scales[:],
+                rhs=z2_codes[:].bitcast(FP8X4),
+                rhs_scale=z2_scales[:],
+                start=True,
+                stop=True,
+            )
+            win = sb(f"win_s{i}", [P, N], F32)
+            nc.scalar.activation(win[:], acc[:], ACT.Copy, scale=0.0625)
+            win_s.append(win)
+
+        out_rows = out_0.rearrange("(p i) v -> p i v", i=PACK)
+        out_words = out_1[0].rearrange("p n t -> p (n t)").bitcast(I32)
+        o_scales = sb("o_scales", [P, N], U8)
+        for h in range(2):
+            cols = slice(HALF * h, HALF * (h + 1))
+            entries = slice(16 * h, 16 * (h + 1))
+            far = sb(f"far{h}", [P, PACK, HALF], F32)
+            res = sb(f"res{h}", [P, PACK, HALF], F32)
+            for i in range(PACK):
+                nc.vector.tensor_scalar(far[:, i, :], win_s[i][:].indirect(l_n6[:, entries]), 0.75, 0.0, ALU.mult, ALU.add)
+            for i in range(PACK):
+                nc.vector.tensor_tensor(res[:, i, :], win_s[i][:].indirect(l_n5[:, entries]), far[:, i, :], ALU.add)
+            nc.sync.dma_start(out_rows[:, :, cols], res[:])
+            res_bf = sb(f"res_bf{h}", [P, PACK * HALF], BF16)
+            dst = res_bf[:].rearrange("p (c j i) -> p c i j", j=4, i=4)
+            src = res[:].rearrange("p i (c j) -> p c i j", j=4)
+            if h == 0:
+                nc.scalar.copy(dst, src)
+            else:
+                nc.vector.tensor_copy(dst, src)
+            o_codes = sb(f"o_codes{h}", [P, HALF], U32)
+            nc.vector.quantize_mx(o_codes[:].bitcast(FP8X4), o_scales[:, cols], res_bf[:])
+            nc.sync.dma_start(out_words[:, cols], o_codes[:].bitcast(I32))
+        scale_rows = out_2[0].bitcast(I32)
+        for q in range(4):
+            queue = nc.scalar if q % 2 else nc.sync
+            queue.dma_start(scale_rows[4 * q : 4 * q + 4, :], o_scales[32 * q : 32 * q + 4, :].bitcast(I32))

@@ -30,13 +30,13 @@ def tile_picked_twknormbkernsum_none_po_kernel(
     nc = tc.nc
     with ExitStack() as ctx:
         keep = ctx.enter_context(tc.tile_pool(name="keep", bufs=1))
-        psum = ctx.enter_context(tc.psum_pool(name="psum", bufs=8))
+        psum = ctx.enter_context(tc.psum_pool(name="psum", bufs=1))
 
-        def sb(name, shape, dtype):
-            return keep.tile(shape, dtype, name=name, align_bytes=64)
+        def sb(name, shape, dtype, tag=None):
+            return keep.tile(shape, dtype, name=name, tag=tag or name, align_bytes=64)
 
-        def bank(name):
-            return psum.tile([P, N], F32, name=name, tag="bank")
+        def bank(name, k):
+            return psum.tile([P, N], F32, name=name, tag=f"bank{k}")
 
         def load_list(name, ap):
             tile = sb(name, [P, N // 16], U16)
@@ -53,9 +53,9 @@ def tile_picked_twknormbkernsum_none_po_kernel(
         ws_raw = [sb(f"ws_raw{i}", [P, N], U8) for i in range(3)]
         for tile in ws_raw:
             nc.gpsimd.memset(tile[:].bitcast(I32), 0)
-        warm = sb("warm", [P, 1], F32)
-        nc.vector.memset(warm[:], 0.0)
-        nc.scalar.activation(warm[:], warm[:], ACT.Exp)
+        half = sb("half", [P, 1], F32)
+        nc.vector.memset(half[:], 1.0)
+        nc.scalar.activation(half[:], half[:], ACT.Copy, scale=0.5)
 
         load_scale_rows(nc.sync, xs, x_scales)
         l_three = load_list("l_three", three)
@@ -68,12 +68,13 @@ def tile_picked_twknormbkernsum_none_po_kernel(
 
         def load_weight(i, words, scales):
             nc.sync.dma_start(ww_raw[i][:].bitcast(I32), words[0].bitcast(I32))
-            load_scale_rows(nc.sync, ws_raw[i], scales)
+            load_scale_rows(nc.scalar if i == 0 else nc.sync, ws_raw[i], scales)
 
         load_weight(0, w3_words, w3_scales)
         l_n3 = load_list("l_n3", n3)
         l_n4 = load_list("l_n4", n4)
         load_weight(1, w2_words, w2_scales)
+        load_weight(2, w1_words, w1_scales)
         gain_rows = sb("gain_rows", [P, P], F32)
         nc.gpsimd.memset(gain_rows[:], 0.0)
         for i, gain in enumerate((ga, gb)):
@@ -81,7 +82,6 @@ def tile_picked_twknormbkernsum_none_po_kernel(
                 gain_rows[4 * i : 4 * i + 4, :].rearrange("t (g r) -> t g r", r=8),
                 gain.rearrange("(g t r) o -> t g (r o)", t=4, r=8),
             )
-        load_weight(2, w1_words, w1_scales)
         l_n2 = load_list("l_n2", n2)
         l_n1 = load_list("l_n1", n1)
         l_n6 = load_list("l_n6", n6)
@@ -91,33 +91,31 @@ def tile_picked_twknormbkernsum_none_po_kernel(
         make_identity(nc, ident[:])
         win_b = [sb(f"win_b{t}", [P, 2 * N], F32) for t in range(PACK)]
         for t in range(PACK):
-            nc.gpsimd.memset(win_b[t][:, N:], 0.0)
+            nc.vector.memset(win_b[t][:, N:], 0.0)
 
-        def pick_scales(name, lst):
-            tile = sb(name, [P, N], U8)
+        def pick_scales(name, lst, tag=None):
+            tile = sb(name, [P, N], U8, tag)
             nc.vector.tensor_copy(tile[:], xs[:].indirect(lst[:]))
             return tile
 
-        def pick_words(name, lst):
-            tile = sb(name, [P, N], U32)
+        def pick_words(name, lst, tag=None):
+            tile = sb(name, [P, N], U32, tag)
             nc.vector.tensor_copy(tile[:], xw[:].indirect(lst[:]))
             return tile
 
-        def deal(i):
-            words = sb(f"ww{i}", [P, 2 * N], U8)
-            scales = sb(f"ws{i}", [P, N], U8)
-            for dst, src in ((words, ww_raw[i]), (scales, ws_raw[i])):
-                nc.vector.tensor_copy(
-                    dst[:].bitcast(I32).rearrange("p (t g e) -> p t g e", t=4, g=16),
-                    src[:].bitcast(I32).rearrange("p (g t e) -> p t g e", t=4, g=16),
-                )
-            return words, scales
+        def deal(engine, name, src, tag=None):
+            dst = sb(name, list(src[:].shape), U8, tag)
+            engine.tensor_copy(
+                dst[:].bitcast(I32).rearrange("p (t g e) -> p t g e", t=4, g=16),
+                src[:].bitcast(I32).rearrange("p (g t e) -> p t g e", t=4, g=16),
+            )
+            return dst
 
-        def project(name, weight, xq, xq_scales):
+        def project(name, first_bank, weight, xq, xq_scales):
             words, scales = weight
             banks = []
             for t in range(PACK):
-                acc = bank(f"{name}{t}")
+                acc = bank(f"{name}{t}", first_bank + t)
                 nc.tensor.matmul_mx(
                     acc[:],
                     lhsT=words[:, 256 * t : 256 * (t + 1)].bitcast(FP4X4),
@@ -132,93 +130,138 @@ def tile_picked_twknormbkernsum_none_po_kernel(
 
         s_three = pick_scales("s_three", l_three)
         s_two = pick_scales("s_two", l_two)
-        s_offs = pick_scales("s_offs", l_offs)
-        w3q = deal(0)
+        s_offs = pick_scales("s_offs", l_offs, None)
+        w3q = deal(nc.gpsimd, "ww0", ww_raw[0]), deal(nc.gpsimd, "ws0", ws_raw[0])
         x_three = pick_words("x_three", l_three)
-        b_ps = project("b", w3q, x_three, s_three)
+        b_ps = project("b", 0, w3q, x_three, s_three)
         for t in range(PACK):
             nc.scalar.copy(win_b[t][:, :N], b_ps[t][:])
 
-        w2q = deal(1)
+        w2q = deal(nc.gpsimd, "ww1", ww_raw[1]), deal(nc.gpsimd, "ws1", ws_raw[1])
         x_two = pick_words("x_two", l_two)
-        d_ps = project("d", w2q, x_two, s_two)
-        w1q = deal(2)
-        x_offs = pick_words("x_offs", l_offs)
+        d_ps = project("d", 4, w2q, x_two, s_two)
 
-        gain_ps = bank("gain_ps")
+        w1q = deal(nc.gpsimd, "ww2", ww_raw[2], None), deal(nc.gpsimd, "ws2", ws_raw[2], None)
+        gain_ps = bank("gain_ps", 0)
         nc.tensor.transpose(gain_ps[:, :P], gain_rows[:], ident[:])
         gains = sb("gains", [P, 8], F32)
-        nc.scalar.activation(gains[:, 0:4], gain_ps[:, 0:4], ACT.Copy, scale=-1.0)
-        nc.scalar.copy(gains[:, 4:8], gain_ps[:, 4:8])
-
-        y_ps = project("y", w1q, x_offs, s_offs)
+        nc.scalar.copy(gains[:], gain_ps[:, : 2 * PACK])
 
         win_d = [sb(f"win_d{t}", [P, 2 * N], F32) for t in range(PACK)]
         win_y = [sb(f"win_y{t}", [P, 2 * N], F32) for t in range(PACK)]
 
-        pa = sb("pa", [P, PACK, N], F32)
-        pb = sb("pb", [P, PACK, N], F32)
-        ka = sb("ka", [P, PACK, N], F32)
-        kb = sb("kb", [P, PACK, N], F32)
-        sq = sb("sq", [P, PACK, N], F32)
+        pa = [sb(f"pa{t}", [P, N], F32) for t in range(PACK)]
+        kern_tile = sb("kern", [P, 2 * PACK, N], F32, "ws_raw2")
+        ka = [kern_tile[:, 2 * t, :] for t in range(PACK)]
+        kb = [kern_tile[:, 2 * t + 1, :] for t in range(PACK)]
+        sq = sb("sq", [P, 2, N], F32)
 
-        def neighbours(picked, kern, lst, t):
-            nc.vector.tensor_copy(picked[:, t, :], win_b[t][:].indirect(lst[:]))
-            nc.vector.tensor_tensor(kern[:, t, :], picked[:, t, :], win_b[t][:, :N], ALU.subtract)
-            nc.scalar.activation(sq[:, t, :], kern[:, t, :], ACT.Square)
-            nc.scalar.activation(kern[:, t, :], sq[:, t, :], ACT.Exp, scale=-0.5)
+        def add_transposed(banks, term, t, c, start, stop):
+            nc.tensor.matmul(
+                banks[c][:, P * t : P * (t + 1)],
+                lhsT=term[t][:, P * c : P * (c + 1)],
+                rhs=ident[:],
+                is_transpose=True,
+                start=start,
+                stop=stop,
+            )
+
+        def neighbours(picked, kern, lst, t, slot):
+            nc.vector.tensor_copy(picked[t][:, :], win_b[t][:].indirect(lst[:]))
+            (nc.gpsimd if 2 * t + slot < 6 else nc.vector).tensor_tensor(kern[t][:, :], picked[t][:, :], win_b[t][:, :N], ALU.subtract)
+            nc.scalar.activation(sq[:, slot, :], kern[t][:, :], ACT.Square)
+            nc.scalar.activation(kern[t][:, :], sq[:, slot, :], ACT.Exp, scale=-0.5)
 
         for t in range(PACK):
             nc.scalar.activation(win_d[t][:, :N], d_ps[t][:], ACT.Abs)
-            nc.scalar.activation(win_d[t ^ 1][:, N:], d_ps[t][:], ACT.Abs)
+            nc.sync.dma_start(win_d[t ^ 1][:, N:], win_d[t][:, :N])
+        x_offs = pick_words("x_offs", l_offs, None)
+        y_ps = project("y", 4, w1q, x_offs, s_offs)
+        weight_ps = [bank(f"weight{c}", c) for c in range(PACK)]
+        def paired(ap):
+            return ap.rearrange("v (u e p) -> v u p e", u=2, e=2)
+
+        pb = []
         for t in range(PACK):
-            neighbours(pa, ka, l_n3, t)
+            pb.append(sb(f"pb{t}", [P, N], F32, None))
+            neighbours(pa, ka, l_n3, t, 0)
+            for c in range(PACK):
+                add_transposed(weight_ps, ka, t, c, t == 0, False)
+            neighbours(pb, kb, l_n4, t, 1)
+            for c in range(PACK):
+                add_transposed(weight_ps, kb, t, c, False, t == PACK - 1)
         for t in range(PACK):
             nc.scalar.activation(win_y[t][:, :N], y_ps[t][:], ACT.Copy, scale=gains[:, t : t + 1])
-            nc.scalar.activation(win_y[t ^ 1][:, N:], y_ps[t][:], ACT.Copy, scale=gains[:, t : t + 1])
-        for t in range(PACK):
-            neighbours(pb, kb, l_n4, t)
+            nc.sync.dma_start(win_y[t ^ 1][:, N:], win_y[t][:, :N])
 
-        den = sb("den", [P, PACK, N], F32)
-        num = sb("num", [P, PACK, N], F32)
+        den = sb("den", [P, PACK, N], F32, None)
         for t in range(PACK):
             nc.vector.tensor_tensor(den[:, t, :], win_d[t][:].indirect(l_n2[:]), win_d[t ^ 1][:, N:], ALU.add)
+        late = sb("late", [P, PACK * N + PACK], F32, "sq")
+        root = late[:, : PACK * N].rearrange("p (t j) -> p t j", t=PACK)
+        minus_gb = late[:, PACK * N :]
+        nc.scalar.activation(minus_gb, gains[:, PACK:], ACT.Copy, scale=-1.0)
+        num = sb("num", [P, PACK, N], F32)
+        mix_ps = [bank(f"mix{c}", 4 + c) for c in range(PACK)]
+        terms_a = [num[:, 0, :], num[:, 1, :], pa[2], pa[3]]
         for t in range(PACK):
-            nc.vector.scalar_tensor_tensor(pa[:, t, :], pa[:, t, :], gains[:, 4 + t : 5 + t], ka[:, t, :], ALU.mult, ALU.mult)
-        nc.vector.tensor_tensor(ka[:], ka[:], kb[:], ALU.add)
-        nc.scalar.activation(ka[:], ka[:], ACT.Abs_reciprocal_sqrt, bias=0.5)
-        nc.scalar.activation(ka[:], ka[:], ACT.Square)
-        nc.scalar.activation(sq[:], den[:], ACT.Abs_reciprocal_sqrt, bias=0.5)
-        nc.scalar.activation(sq[:], sq[:], ACT.Square)
-        for t in range(PACK):
-            nc.vector.scalar_tensor_tensor(pb[:, t, :], pb[:, t, :], gains[:, 4 + t : 5 + t], kb[:, t, :], ALU.mult, ALU.mult)
-        nc.vector.tensor_tensor(pa[:], pa[:], pb[:], ALU.add)
+            for k, (term, picked, kern) in enumerate(((terms_a, pa, ka), (pb, pb, kb))):
+                nc.vector.scalar_tensor_tensor(
+                    term[t][:, :], picked[t][:, :], minus_gb[:, t : t + 1], kern[t][:, :], ALU.mult, ALU.mult
+                )
+                for c in range(PACK):
+                    add_transposed(mix_ps, term, t, c, t == 0 and k == 0, t == PACK - 1 and k == 1)
+        inv_low = sb("inv_low", [P, 2, N], F32)
+        inv_weight = [inv_low[:], num[:, 2:, :]]
+        for c in range(PACK):
+            nc.scalar.activation(
+                root[:, c, :].rearrange("v (u p e) -> v u p e", u=2, e=2), paired(weight_ps[c][:]), ACT.Abs_reciprocal_sqrt, bias=half[:]
+            )
+            nc.scalar.activation(inv_weight[c // 2][:, c % 2, :], root[:, c, :], ACT.Square)
+        z2t = [sb(f"z2t{c}", [P, N], BF16) for c in range(PACK)]
+        for c in range(PACK):
+            nc.vector.tensor_tensor(
+                z2t[c][:].rearrange("v (u p e) -> v u p e", u=2, e=2),
+                paired(mix_ps[c][:]),
+                inv_weight[c // 2][:, c % 2, :].rearrange("v (u p e) -> v u p e", u=2, e=2),
+                ALU.mult,
+            )
+        nc.scalar.activation(root, den[:], ACT.Abs_reciprocal_sqrt, bias=half[:])
+        nc.scalar.activation(den[:], root, ACT.Square)
+        z2_bf = sb("z2_bf", [P, PACK * N], BF16, "sq")
+        for h in range(2):
+            back = bank(f"back{h}", h)
+            for k in range(2):
+                for u in range(2):
+                    nc.tensor.transpose(
+                        back[:, P * (2 * k + u) : P * (2 * k + u + 1)],
+                        z2t[2 * h + k][:].bitcast(F32)[:, P * u : P * (u + 1)],
+                        ident[:],
+                    )
+            nc.scalar.copy(
+                z2_bf[:].bitcast(F32)[:, N * h : N * (h + 1)].rearrange("p (k v u) -> p k v u", k=2, u=2),
+                back[:].rearrange("p (k u v) -> p k v u", k=2, u=2),
+            )
         for t in range(PACK):
             nc.vector.tensor_tensor(num[:, t, :], win_y[t][:].indirect(l_n1[:]), win_y[t ^ 1][:, N:], ALU.subtract)
 
-        z2_bf = sb("z2_bf", [P, PACK * N], BF16)
-        nc.vector.tensor_tensor(
-            z2_bf[:].rearrange("p (c i t) -> p c t i", i=4, t=4),
-            pa[:].rearrange("p t (c i) -> p c t i", i=4),
-            ka[:].rearrange("p t (c i) -> p c t i", i=4),
-            ALU.mult,
-        )
-        z_bf = sb("z_bf", [P, PACK * N], BF16)
-        nc.vector.tensor_tensor(
-            z_bf[:].rearrange("p (i c t) -> p c t i", i=4, t=4),
-            num[:].rearrange("p t (c i) -> p c t i", i=4),
-            sq[:].rearrange("p t (c i) -> p c t i", i=4),
-            ALU.mult,
-        )
         z2_codes = sb("z2_codes", [P, N], U32)
         z2_scales = sb("z2_scales", [P, N], U8)
         nc.vector.quantize_mx(z2_codes[:].bitcast(FP8X4), z2_scales[:], z2_bf[:])
         win_s = []
         for i in range(PACK):
+            if i % 2 == 0:
+                z_bf = sb(f"z_bf{i}", [P, 2 * N], BF16, "sq" if i else None)
+                nc.vector.tensor_tensor(
+                    z_bf[:].rearrange("p (i c t) -> p c t i", i=2, t=4),
+                    num[:].rearrange("p t (c i) -> p c t i", i=4)[:, :, :, i : i + 2],
+                    den[:].rearrange("p t (c i) -> p c t i", i=4)[:, :, :, i : i + 2],
+                    ALU.mult,
+                )
             z_codes = sb(f"z_codes{i}", [P, P], U32)
             z_scales = sb(f"z_scales{i}", [P, P], U8)
-            nc.vector.quantize_mx(z_codes[:].bitcast(FP8X4), z_scales[:], z_bf[:, N * i : N * (i + 1)])
-            acc = bank(f"s{i}")
+            nc.vector.quantize_mx(z_codes[:].bitcast(FP8X4), z_scales[:], z_bf[:, N * (i % 2) : N * (i % 2 + 1)])
+            acc = bank(f"s{i}", 4 + i)
             nc.tensor.matmul_mx(
                 acc[:],
                 lhsT=z_codes[:].bitcast(FP8X4),
@@ -238,13 +281,13 @@ def tile_picked_twknormbkernsum_none_po_kernel(
         for h in range(2):
             cols = slice(HALF * h, HALF * (h + 1))
             entries = slice(16 * h, 16 * (h + 1))
-            far = sb(f"far{h}", [P, PACK, HALF], F32)
-            res = sb(f"res{h}", [P, PACK, HALF], F32)
+            far = sb(f"far{h}", [P, PACK, HALF], F32, "far")
+            res = sb(f"res{h}", [P, PACK, HALF], F32, None if h else "z_codes3")
             for i in range(PACK):
                 nc.vector.tensor_scalar(far[:, i, :], win_s[i][:].indirect(l_n6[:, entries]), 0.75, 0.0, ALU.mult, ALU.add)
             for i in range(PACK):
                 nc.vector.tensor_tensor(res[:, i, :], win_s[i][:].indirect(l_n5[:, entries]), far[:, i, :], ALU.add)
-            nc.sync.dma_start(out_rows[:, :, cols], res[:])
+                nc.sync.dma_start(out_rows[:, i, cols], res[:, i, :])
             res_bf = sb(f"res_bf{h}", [P, PACK * HALF], BF16)
             dst = res_bf[:].rearrange("p (c j i) -> p c i j", j=4, i=4)
             src = res[:].rearrange("p i (c j) -> p c i j", j=4)

from contextlib import ExitStack

import concourse.mybir as mybir
from concourse.masks import make_identity

F32 = mybir.dt.float32
BF16 = mybir.dt.bfloat16
I32 = mybir.dt.int32
U32 = mybir.dt.uint32
U16 = mybir.dt.uint16
U8 = mybir.dt.uint8
FP8X4 = mybir.dt.float8_e4m3fn_x4
FP4X4 = mybir.dt.float4_e2m1fn_x4
ACT = mybir.ActivationFunctionType
ALU = mybir.AluOpType

P = 128
N = 512
T = 2048
PACK = 4
HALF = N // 2

FLOPS = 4 * 2 * N * N * N


def tile_picked_twknormbkernsum_none_po_kernel(
    tc, x_words, x_scales, w1_words, w1_scales, w2_words, w2_scales, w3_words, w3_scales,
    ga, gb, offs, two, n1, n2, three, n3, n4, n5, n6, out_0, out_1, out_2,
):
    nc = tc.nc
    with ExitStack() as ctx:
        keep = ctx.enter_context(tc.tile_pool(name="keep", bufs=1))
        psum = ctx.enter_context(tc.psum_pool(name="psum", bufs=1))

        def sb(name, shape, dtype, tag=None):
            return keep.tile(shape, dtype, name=name, tag=tag or name, align_bytes=64)

        def bank(name, k):
            return psum.tile([P, N], F32, name=name, tag=f"bank{k}")

        def load_list(name, ap):
            tile = sb(name, [P, N // 16], U16)
            nc.sync.dma_start(tile[:], ap)
            return tile

        def load_scale_rows(queue, tile, scales):
            rows = scales[0].bitcast(I32)
            for q in range(4):
                queue.dma_start(tile[32 * q : 32 * q + 4, :].bitcast(I32), rows[4 * q : 4 * q + 4, :])

        xs = sb("xs", [P, T], U8)
        nc.gpsimd.memset(xs[:].bitcast(I32), 0)
        ws_raw = [sb(f"ws_raw{i}", [P, N], U8) for i in range(3)]
        for tile in ws_raw:
            nc.gpsimd.memset(tile[:].bitcast(I32), 0)
        half = sb("half", [P, 1], F32)
        nc.vector.memset(half[:], 1.0)
        nc.scalar.activation(half[:], half[:], ACT.Copy, scale=0.5)

        load_scale_rows(nc.sync, xs, x_scales)
        l_three = load_list("l_three", three)
        l_two = load_list("l_two", two)
        l_offs = load_list("l_offs", offs)
        xw = sb("xw", [P, T], U32)
        nc.sync.dma_start(xw[:].bitcast(I32), x_words[0].rearrange("p n t -> p (n t)").bitcast(I32))

        ww_raw = [sb(f"ww_raw{i}", [P, 2 * N], U8) for i in range(3)]

        def load_weight(i, words, scales):
            nc.sync.dma_start(ww_raw[i][:].bitcast(I32), words[0].bitcast(I32))
            load_scale_rows(nc.scalar if i == 0 else nc.sync, ws_raw[i], scales)

        load_weight(0, w3_words, w3_scales)
        l_n3 = load_list("l_n3", n3)
        l_n4 = load_list("l_n4", n4)
        load_weight(1, w2_words, w2_scales)
        load_weight(2, w1_words, w1_scales)
        gain_rows = sb("gain_rows", [P, P], F32)
        nc.gpsimd.memset(gain_rows[:], 0.0)
        for i, gain in enumerate((ga, gb)):
            nc.sync.dma_start(
                gain_rows[4 * i : 4 * i + 4, :].rearrange("t (g r) -> t g r", r=8),
                gain.rearrange("(g t r) o -> t g (r o)", t=4, r=8),
            )
        l_n2 = load_list("l_n2", n2)
        l_n1 = load_list("l_n1", n1)
        l_n6 = load_list("l_n6", n6)
        l_n5 = load_list("l_n5", n5)

        ident = sb("ident", [P, P], F32)
        make_identity(nc, ident[:])
        win_b = [sb(f"win_b{t}", [P, 2 * N], F32) for t in range(PACK)]
        for t in range(PACK):
            nc.vector.memset(win_b[t][:, N:], 0.0)

        def pick_scales(name, lst, tag=None):
            tile = sb(name, [P, N], U8, tag)
            nc.vector.tensor_copy(tile[:], xs[:].indirect(lst[:]))
            return tile

        def pick_words(name, lst, tag=None):
            tile = sb(name, [P, N], U32, tag)
            nc.vector.tensor_copy(tile[:], xw[:].indirect(lst[:]))
            return tile

        def deal(engine, name, src, tag=None):
            dst = sb(name, list(src[:].shape), U8, tag)
            engine.tensor_copy(
                dst[:].bitcast(I32).rearrange("p (t g e) -> p t g e", t=4, g=16),
                src[:].bitcast(I32).rearrange("p (g t e) -> p t g e", t=4, g=16),
            )
            return dst

        def project(name, first_bank, weight, xq, xq_scales):
            words, scales = weight
            banks = []
            for t in range(PACK):
                acc = bank(f"{name}{t}", first_bank + t)
                nc.tensor.matmul_mx(
                    acc[:],
                    lhsT=words[:, 256 * t : 256 * (t + 1)].bitcast(FP4X4),
                    lhsT_scale=scales[:, P * t : P * (t + 1)],
                    rhs=xq[:].bitcast(FP8X4),
                    rhs_scale=xq_scales[:],
                    start=True,
                    stop=True,
                )
                banks.append(acc)
            return banks

        s_three = pick_scales("s_three", l_three)
        s_two = pick_scales("s_two", l_two)
        s_offs = pick_scales("s_offs", l_offs, None)
        w3q = deal(nc.gpsimd, "ww0", ww_raw[0]), deal(nc.gpsimd, "ws0", ws_raw[0])
        x_three = pick_words("x_three", l_three)
        b_ps = project("b", 0, w3q, x_three, s_three)
        for t in range(PACK):
            nc.scalar.copy(win_b[t][:, :N], b_ps[t][:])

        w2q = deal(nc.gpsimd, "ww1", ww_raw[1]), deal(nc.gpsimd, "ws1", ws_raw[1])
        x_two = pick_words("x_two", l_two)
        d_ps = project("d", 4, w2q, x_two, s_two)

        w1q = deal(nc.gpsimd, "ww2", ww_raw[2], None), deal(nc.gpsimd, "ws2", ws_raw[2], None)
        gain_ps = bank("gain_ps", 0)
        nc.tensor.transpose(gain_ps[:, :P], gain_rows[:], ident[:])
        gains = sb("gains", [P, 8], F32)
        nc.scalar.copy(gains[:], gain_ps[:, : 2 * PACK])

        win_d = [sb(f"win_d{t}", [P, 2 * N], F32) for t in range(PACK)]
        win_y = [sb(f"win_y{t}", [P, 2 * N], F32) for t in range(PACK)]

        pa = [sb(f"pa{t}", [P, N], F32) for t in range(PACK)]
        kern_tile = sb("kern", [P, 2 * PACK, N], F32, "ws_raw2")
        ka = [kern_tile[:, 2 * t, :] for t in range(PACK)]
        kb = [kern_tile[:, 2 * t + 1, :] for t in range(PACK)]
        sq = sb("sq", [P, 2, N], F32)

        def add_transposed(banks, term, t, c, start, stop):
            nc.tensor.matmul(
                banks[c][:, P * t : P * (t + 1)],
                lhsT=term[t][:, P * c : P * (c + 1)],
                rhs=ident[:],
                is_transpose=True,
                start=start,
                stop=stop,
            )

        def neighbours(picked, kern, lst, t, slot):
            nc.vector.tensor_copy(picked[t][:, :], win_b[t][:].indirect(lst[:]))
            (nc.gpsimd if 2 * t + slot < 6 else nc.vector).tensor_tensor(kern[t][:, :], picked[t][:, :], win_b[t][:, :N], ALU.subtract)
            nc.scalar.activation(sq[:, slot, :], kern[t][:, :], ACT.Square)
            nc.scalar.activation(kern[t][:, :], sq[:, slot, :], ACT.Exp, scale=-0.5)

        for t in range(PACK):
            nc.scalar.activation(win_d[t][:, :N], d_ps[t][:], ACT.Abs)
            nc.sync.dma_start(win_d[t ^ 1][:, N:], win_d[t][:, :N])
        x_offs = pick_words("x_offs", l_offs, None)
        y_ps = project("y", 4, w1q, x_offs, s_offs)
        weight_ps = [bank(f"weight{c}", c) for c in range(PACK)]
        def paired(ap):
            return ap.rearrange("v (u e p) -> v u p e", u=2, e=2)

        pb = []
        for t in range(PACK):
            pb.append(sb(f"pb{t}", [P, N], F32, None))
            neighbours(pa, ka, l_n3, t, 0)
            for c in range(PACK):
                add_transposed(weight_ps, ka, t, c, t == 0, False)
            neighbours(pb, kb, l_n4, t, 1)
            for c in range(PACK):
                add_transposed(weight_ps, kb, t, c, False, t == PACK - 1)
        for t in range(PACK):
            nc.scalar.activation(win_y[t][:, :N], y_ps[t][:], ACT.Copy, scale=gains[:, t : t + 1])
            nc.sync.dma_start(win_y[t ^ 1][:, N:], win_y[t][:, :N])

        den = sb("den", [P, PACK, N], F32, None)
        for t in range(PACK):
            nc.vector.tensor_tensor(den[:, t, :], win_d[t][:].indirect(l_n2[:]), win_d[t ^ 1][:, N:], ALU.add)
        late = sb("late", [P, PACK * N + PACK], F32, "sq")
        root = late[:, : PACK * N].rearrange("p (t j) -> p t j", t=PACK)
        minus_gb = late[:, PACK * N :]
        nc.scalar.activation(minus_gb, gains[:, PACK:], ACT.Copy, scale=-1.0)
        num = sb("num", [P, PACK, N], F32)
        mix_ps = [bank(f"mix{c}", 4 + c) for c in range(PACK)]
        terms_a = [num[:, 0, :], num[:, 1, :], pa[2], pa[3]]
        for t in range(PACK):
            for k, (term, picked, kern) in enumerate(((terms_a, pa, ka), (pb, pb, kb))):
                nc.vector.scalar_tensor_tensor(
                    term[t][:, :], picked[t][:, :], minus_gb[:, t : t + 1], kern[t][:, :], ALU.mult, ALU.mult
                )
                for c in range(PACK):
                    add_transposed(mix_ps, term, t, c, t == 0 and k == 0, t == PACK - 1 and k == 1)
        inv_low = sb("inv_low", [P, 2, N], F32)
        inv_weight = [inv_low[:], num[:, 2:, :]]
        for c in range(PACK):
            nc.scalar.activation(
                root[:, c, :].rearrange("v (u p e) -> v u p e", u=2, e=2), paired(weight_ps[c][:]), ACT.Abs_reciprocal_sqrt, bias=half[:]
            )
            nc.scalar.activation(inv_weight[c // 2][:, c % 2, :], root[:, c, :], ACT.Square)
        z2t = [sb(f"z2t{c}", [P, N], BF16) for c in range(PACK)]
        for c in range(PACK):
            nc.vector.tensor_tensor(
                z2t[c][:].rearrange("v (u p e) -> v u p e", u=2, e=2),
                paired(mix_ps[c][:]),
                inv_weight[c // 2][:, c % 2, :].rearrange("v (u p e) -> v u p e", u=2, e=2),
                ALU.mult,
            )
        nc.scalar.activation(root, den[:], ACT.Abs_reciprocal_sqrt, bias=half[:])
        nc.scalar.activation(den[:], root, ACT.Square)
        z2_bf = sb("z2_bf", [P, PACK * N], BF16, "sq")
        for h in range(2):
            back = bank(f"back{h}", h)
            for k in range(2):
                for u in range(2):
                    nc.tensor.transpose(
                        back[:, P * (2 * k + u) : P * (2 * k + u + 1)],
                        z2t[2 * h + k][:].bitcast(F32)[:, P * u : P * (u + 1)],
                        ident[:],
                    )
            nc.scalar.copy(
                z2_bf[:].bitcast(F32)[:, N * h : N * (h + 1)].rearrange("p (k v u) -> p k v u", k=2, u=2),
                back[:].rearrange("p (k u v) -> p k v u", k=2, u=2),
            )
        for t in range(PACK):
            nc.vector.tensor_tensor(num[:, t, :], win_y[t][:].indirect(l_n1[:]), win_y[t ^ 1][:, N:], ALU.subtract)

        z2_codes = sb("z2_codes", [P, N], U32)
        z2_scales = sb("z2_scales", [P, N], U8)
        nc.vector.quantize_mx(z2_codes[:].bitcast(FP8X4), z2_scales[:], z2_bf[:])
        win_s = []
        for i in range(PACK):
            if i % 2 == 0:
                z_bf = sb(f"z_bf{i}", [P, 2 * N], BF16, "sq" if i else None)
                nc.vector.tensor_tensor(
                    z_bf[:].rearrange("p (i c t) -> p c t i", i=2, t=4),
                    num[:].rearrange("p t (c i) -> p c t i", i=4)[:, :, :, i : i + 2],
                    den[:].rearrange("p t (c i) -> p c t i", i=4)[:, :, :, i : i + 2],
                    ALU.mult,
                )
            z_codes = sb(f"z_codes{i}", [P, P], U32)
            z_scales = sb(f"z_scales{i}", [P, P], U8)
            nc.vector.quantize_mx(z_codes[:].bitcast(FP8X4), z_scales[:], z_bf[:, N * (i % 2) : N * (i % 2 + 1)])
            acc = bank(f"s{i}", 4 + i)
            nc.tensor.matmul_mx(
                acc[:],
                lhsT=z_codes[:].bitcast(FP8X4),
                lhsT_scale=z_scales[:],
                rhs=z2_codes[:].bitcast(FP8X4),
                rhs_scale=z2_scales[:],
                start=True,
                stop=True,
            )
            win = sb(f"win_s{i}", [P, N], F32)
            nc.scalar.activation(win[:], acc[:], ACT.Copy, scale=0.0625)
            win_s.append(win)

        out_rows = out_0.rearrange("(p i) v -> p i v", i=PACK)
        out_words = out_1[0].rearrange("p n t -> p (n t)").bitcast(I32)
        o_scales = sb("o_scales", [P, N], U8)
        for h in range(2):
            cols = slice(HALF * h, HALF * (h + 1))
            entries = slice(16 * h, 16 * (h + 1))
            far = sb(f"far{h}", [P, PACK, HALF], F32, "far")
            res = sb(f"res{h}", [P, PACK, HALF], F32, None if h else "z_codes3")
            for i in range(PACK):
                nc.vector.tensor_scalar(far[:, i, :], win_s[i][:].indirect(l_n6[:, entries]), 0.75, 0.0, ALU.mult, ALU.add)
            for i in range(PACK):
                nc.vector.tensor_tensor(res[:, i, :], win_s[i][:].indirect(l_n5[:, entries]), far[:, i, :], ALU.add)
                nc.sync.dma_start(out_rows[:, i, cols], res[:, i, :])
            res_bf = sb(f"res_bf{h}", [P, PACK * HALF], BF16)
            dst = res_bf[:].rearrange("p (c j i) -> p c i j", j=4, i=4)
            src = res[:].rearrange("p i (c j) -> p c i j", j=4)
            if h == 0:
                nc.scalar.copy(dst, src)
            else:
                nc.vector.tensor_copy(dst, src)
            o_codes = sb(f"o_codes{h}", [P, HALF], U32)
            nc.vector.quantize_mx(o_codes[:].bitcast(FP8X4), o_scales[:, cols], res_bf[:])
            nc.sync.dma_start(out_words[:, cols], o_codes[:].bitcast(I32))
        scale_rows = out_2[0].bitcast(I32)
        for q in range(4):
            queue = nc.scalar if q % 2 else nc.sync
            queue.dma_start(scale_rows[4 * q : 4 * q + 4, :], o_scales[32 * q : 32 * q + 4, :].bitcast(I32))
